import numpy as np
import ml_dtypes


def mxq(x, axis, fmt="e4m3"):
    dtype, down = {"e4m3": (ml_dtypes.float8_e4m3fn, 7), "e5m2": (ml_dtypes.float8_e5m2, 14)}[fmt]
    v = np.moveaxis(np.asarray(x, np.float32).astype(ml_dtypes.bfloat16).astype(np.float64), axis, -1)
    blocks = v.reshape(v.shape[:-1] + (-1, 32))
    amax = np.abs(blocks).max(-1, keepdims=True)
    byte = np.maximum(np.where(amax > 0, np.frexp(amax)[1] - 1 + 127, 0) - down, 1)
    scale = np.exp2(byte - 127.0)
    codes = (blocks / scale).astype(np.float32).astype(dtype).astype(np.float64)
    return np.moveaxis((codes * scale).reshape(v.shape), -1, axis)


WIDE = False


def mx_kscale(k):
    if not WIDE:
        return np.ones(k)
    levels = np.array([10, -10, 5, -5, 0])
    if k % 512:
        return np.exp2(np.random.permutation(np.resize(levels, k // 32))).repeat(32)
    a = np.empty((k // 512, 16))
    for p in range(k // 512):
        a[p, :8] = np.random.permutation(np.resize(levels, 8))
        for g in range(8):
            far = levels[np.abs(levels - a[p, g]) >= 10]
            a[p, g + 8] = far[np.random.randint(len(far))]
    return np.exp2(a.ravel()).repeat(32)


def f64(x):
    return np.asarray(x).astype(np.float64)


def striped8(idx):
    return np.concatenate([x.reshape(-1, 16).T for x in idx]).astype(np.uint16)


def runs(offs, k):
    lists = np.stack([offs[16 * r : 16 * r + 16].T.reshape(-1) for r in range(8)]).astype(np.int64)
    return lists[np.arange(k) % 512 // 64]


def pack_weight(w):
    k, n = w.shape
    w = f64(np.asarray(w, np.float32).astype(ml_dtypes.bfloat16)).reshape(k // 32, 32, n)
    amax = np.abs(w).max(1)
    byte = np.clip(np.where(amax > 0, np.frexp(amax)[1] - 1 + 127 - 7, 1), 1, 254)
    scaled = (w * np.exp2(127.0 - byte)[:, None, :]).reshape(k, n).astype(np.float32)
    words = np.ascontiguousarray(scaled.reshape(k // 512, 128, 4, n).transpose(0, 1, 3, 2)).astype(ml_dtypes.float8_e4m3fn).view(np.uint8)
    return words, np.ascontiguousarray(byte.astype(np.uint8).reshape(k // 512, 16, n))


def unpack_weight(words, scales):
    g, p, n, _ = words.shape
    vals = np.ascontiguousarray(words).view(ml_dtypes.float8_e4m3fn).astype(np.float64) * np.repeat(np.exp2(scales.astype(np.float64) - 127.0), 8, axis=1)[..., None]
    return vals.transpose(0, 1, 3, 2).reshape(g * 512, n)


E2M1 = np.array([0.0, 0.5, 1.0, 1.5, 2.0, 3.0, 4.0, 6.0, -0.0, -0.5, -1.0, -1.5, -2.0, -3.0, -4.0, -6.0])


def pack_fp4(w):
    k, n = w.shape
    w = f64(np.asarray(w, np.float32).astype(ml_dtypes.bfloat16)).reshape(k // 32, 32, n)
    amax = np.abs(w).max(1)
    mant, ex = np.frexp(amax / 6.0)
    byte = np.clip(np.where(amax > 0, np.where(mant > 0.5, ex, ex - 1) + 127, 1), 1, 254)
    scaled = (w * np.exp2(127.0 - byte)[:, None, :]).reshape(k, n).astype(np.float32)
    c = np.ascontiguousarray(scaled.reshape(k // 512, 128, 4, n).transpose(0, 1, 3, 2)).astype(ml_dtypes.float4_e2m1fn).view(np.uint8) & 0xF
    words = (c[..., 0::2] | (c[..., 1::2] << 4)).reshape(k // 512, 128, 2 * n)
    return np.ascontiguousarray(words), np.ascontiguousarray(byte.astype(np.uint8).reshape(k // 512, 16, n))


def unpack_fp4(words, scales):
    g, _, n = scales.shape
    words = np.ascontiguousarray(words).reshape(g, 128, n, 2)
    nib = np.empty((g, 128, n, 4), np.uint8)
    nib[..., 0::2] = words & 0xF
    nib[..., 1::2] = words >> 4
    vals = E2M1[nib] * np.repeat(np.exp2(scales.astype(np.float64) - 127.0), 8, axis=1)[..., None]
    return vals.transpose(0, 1, 3, 2).reshape(g * 512, n)


K, T, S, H, G = 512, 2048, 512, 512, 2048


def setup_inputs():
    n = np.random.standard_normal
    s = mx_kscale(K)[:, None]
    packed_xT = pack_weight(n((K, T)) * s)
    packed_w1 = pack_fp4(n((K, H)) / np.sqrt(K) / s)
    packed_dT = pack_weight(n((K, G)) / s)
    return {
        "x_words": packed_xT[0],
        "x_scales": packed_xT[1],
        "w1_words": packed_w1[0],
        "w1_scales": packed_w1[1],
        "gs": (np.random.uniform(0.5, 1.5, (K, 1)) * s).astype(np.float32),
        "d_words": packed_dT[0],
        "d_scales": packed_dT[1],
        "offs": striped8(np.random.randint(0, T, (8, S))),
        "n1": striped8(np.stack([np.random.permutation(S) for _ in range(8)])),
        "n2": striped8(np.stack([np.random.permutation(S) for _ in range(8)])),
        "ka": striped8(np.random.randint(0, G, (8, H))),
        "kb": striped8(np.random.randint(0, G, (8, H))),
        "n3": striped8(np.stack([np.random.permutation(S) for _ in range(8)])),
        "n4": striped8(np.stack([np.random.permutation(S) for _ in range(8)])),
    }


def reference(x_words, x_scales, w1_words, w1_scales, gs, d_words, d_scales, offs, n1, n2, ka, kb, n3, n4):
    d_ka = unpack_weight(d_words, d_scales)[np.arange(K)[:, None], runs(ka, K)]
    xq = unpack_weight(x_words, x_scales)[np.arange(K)[:, None], runs(offs, K)]
    y = unpack_fp4(w1_words, w1_scales).T @ xq
    ds = np.zeros((H, S))
    ds[np.arange(H)[:, None], runs(n1, H)] = y
    z = f64(gs) * (np.maximum(y, ds[np.arange(H)[:, None], runs(n2, H)]))
    zq = mxq(z, 0, "e4m3")
    d_kb = unpack_weight(d_words, d_scales)[np.arange(K)[:, None], runs(kb, K)]
    h = 0.0625 * (d_ka.T @ zq + d_kb.T @ zq)
    ds2 = np.zeros((H, S))
    ds2[np.arange(H)[:, None], runs(n3, H)] = h
    ds3 = np.zeros((H, S))
    ds3[np.arange(H)[:, None], runs(n4, H)] = h
    return np.maximum(ds2, ds3)

@@ -1,0 +1,263 @@
+from contextlib import ExitStack
+
+import concourse.mybir as mybir
+
+F32 = mybir.dt.float32
+BF16 = mybir.dt.bfloat16
+I32 = mybir.dt.int32
+U32 = mybir.dt.uint32
+U16 = mybir.dt.uint16
+U8 = mybir.dt.uint8
+FP8X4 = mybir.dt.float8_e4m3fn_x4
+FP4X4 = mybir.dt.float4_e2m1fn_x4
+COPY = mybir.ActivationFunctionType.Copy
+MAX = mybir.AluOpType.max
+
+P = 128
+S = 512
+TABLE = 2048
+HALF = 256
+QUARTER = 128
+FLOPS = 3 * 2 * 512 * 512 * 512
+
+
+def tile_picked_hdaqrelaysendtwo_none_p_kernel(tc, x_words, x_scales, w1_words, w1_scales, gs, d_words, d_scales, offs, n1, n2, ka, kb, n3, n4, out):
+    nc = tc.nc
+    with ExitStack() as ctx:
+        lists = ctx.enter_context(tc.tile_pool(name="lists", bufs=1))
+        sb = ctx.enter_context(tc.tile_pool(name="sb", bufs=1))
+        ps = ctx.enter_context(tc.psum_pool(name="ps", bufs=1))
+
+        def load_list(src, name):
+            t = lists.tile([P, S // 16], U16, name=name)
+            nc.sync.dma_start(t[:], src)
+            return t
+
+        def entries(lst, a, n):
+            return lst[:, a // 16 : (a + n) // 16]
+
+        def load_scale_table(src, name, queue):
+            t = sb.tile([P, TABLE], U8, name=name, tag=name, align_bytes=64)
+            rows = src[0].bitcast(I32)
+            queue.dma_start(t[:].bitcast(I32), rows.unsqueeze(1).to_broadcast([16, 8, TABLE // 4]))
+            return t
+
+        def load_word_table(src, name, tag):
+            t = sb.tile([P, TABLE], I32, name=name, tag=tag, align_bytes=64)
+            nc.sync.dma_start(t[:], src[0].rearrange("p n t -> p (n t)").bitcast(I32))
+            return t
+
+        l_offs = load_list(offs, "l_offs")
+        xs_table = load_scale_table(x_scales, "xs_table", nc.scalar)
+        l_ka = load_list(ka, "l_ka")
+        w1s_raw = sb.tile([P, S], U8, name="w1s_raw", align_bytes=64)
+        w1s_rows = w1_scales[0].bitcast(I32).rearrange("(q i) c -> i q c", i=4)
+        for i in range(4):
+            nc.gpsimd.dma_start(w1s_raw[i:P:4, :].bitcast(I32), w1s_rows[i].unsqueeze(1).to_broadcast([4, 8, S // 4]))
+        ds_table = load_scale_table(d_scales, "ds_table", nc.scalar)
+        l_kb = load_list(kb, "l_kb")
+        w1w_raw = sb.tile([P, 2 * S], U8, name="w1w_raw", align_bytes=64)
+        nc.scalar.dma_start(w1w_raw[:].bitcast(I32), w1_words[0].bitcast(I32))
+        l_n1 = load_list(n1, "l_n1")
+        xw_table = load_word_table(x_words, "xw_table", "xw_table")
+
+        xs_picked = sb.tile([P, S], U8, name="xs_picked", tag="xs_picked", align_bytes=64)
+        xs_plane = sb.tile([P, S], U8, name="xs_plane", align_bytes=64)
+        nc.vector.memset(xs_plane[:].bitcast(I32), 0)
+        nc.vector.tensor_copy(xs_picked[:], xs_table[:].indirect(l_offs[:]))
+        w1w = sb.tile([P, 2 * S], U8, name="w1w", align_bytes=64)
+        for i in range(4):
+            nc.scalar.dma_start(xs_plane[i:P:32, :].bitcast(I32), xs_picked[8 * i : P : 32, :].bitcast(I32))
+        nc.scalar.copy(w1w[:].bitcast(U16).rearrange("p (t m) -> p t m", t=4), w1w_raw[:].bitcast(U16).rearrange("p (m t) -> p t m", t=4))
+        w1s = sb.tile([P, S], U8, name="w1s", align_bytes=64)
+        nc.vector.tensor_copy(w1s[:].rearrange("p (t m) -> p m t", t=4), w1s_raw[:].rearrange("p (m t) -> p m t", t=4))
+
+        l_n2 = load_list(n2, "l_n2")
+        l_n3 = load_list(n3, "l_n3")
+        l_n4 = load_list(n4, "l_n4")
+        dw_table = load_word_table(d_words, "dw_table", "xs_table")
+        gs_sb = sb.tile([P, 4], F32, name="gs_sb", tag="xs_picked", align_bytes=64)
+        nc.sync.dma_start(gs_sb[:], gs.rearrange("(p t) o -> p (t o)", t=4))
+
+        xw = sb.tile([P, S], U32, name="xw", align_bytes=64)
+        for a in (0, HALF):
+            nc.vector.tensor_copy(xw[:, a : a + HALF], xw_table[:].bitcast(U32).indirect(entries(l_offs, a, HALF)))
+
+        d_plane = sb.tile([P, 2 * S], U8, name="d_plane", align_bytes=64)
+        for j, lst in enumerate((l_ka, l_kb)):
+            picked = sb.tile([P, S], U8, name=f"ds_picked{j}", tag=("ds_picked0", "xw_table")[j], align_bytes=64)
+            nc.vector.tensor_copy(picked[:], ds_table[:].indirect(lst[:]))
+            nc.vector.tensor_copy(
+                d_plane[:, j * S : (j + 1) * S].bitcast(I32).rearrange("p (t g b) -> p t g b", t=4, b=2),
+                picked[:].bitcast(I32).rearrange("p (g t b) -> p t g b", t=4, b=2),
+            )
+        for i in range(1, 4):
+            nc.sync.dma_start(d_plane[i:P:32, :].bitcast(I32), d_plane[8 * i : P : 32, :].bitcast(I32))
+
+        y_ps = [ps.tile([P, S], F32, name=f"bank{t}") for t in range(4)]
+        z_bf = sb.tile([P, S, 4], BF16, name="z_bf", align_bytes=64)
+        larger = [sb.tile([P, S], F32, name=f"larger{t}") for t in range(4)]
+
+        def buf(shape, dtype, name, tag=None):
+            return sb.tile(shape, dtype, name=name, tag=tag or name, align_bytes=64)
+
+        def project(t, h, tag=None):
+            cols = slice(h * HALF, (h + 1) * HALF)
+            nc.tensor.matmul_mx(
+                out=y_ps[t][:, cols],
+                lhsT=w1w[:, t * 256 : (t + 1) * 256].bitcast(FP4X4),
+                lhsT_scale=w1s[:, t * P : (t + 1) * P],
+                rhs=xw[:, cols].bitcast(FP8X4),
+                rhs_scale=xs_plane[:, cols],
+                start=True,
+                stop=True,
+            )
+            y_sb = buf([P, HALF], F32, f"y{t}{h}", tag)
+            nc.scalar.activation(y_sb[:], y_ps[t][:, cols], COPY)
+            return y_sb
+
+        def send(sent, y_sb, h):
+            nc.vector.tensor_copy(sent[:].indirect(entries(l_n1, h * HALF, HALF)), y_sb[:])
+
+        def fetch(sent, dst, a, n):
+            nc.scalar.activation(dst, sent[:].indirect(entries(l_n2, a, n)), COPY)
+
+        def take_larger(t, fetched, a, n, dst=None):
+            dst = larger[t][:, a : a + n] if dst is None else dst
+            nc.vector.tensor_tensor(dst, fetched, y_ps[t][:, a : a + n], MAX)
+
+        def weigh(t, a, n, src=None):
+            src = larger[t][:, a : a + n] if src is None else src
+            nc.scalar.activation(z_bf[:, a : a + n, t], src, COPY, scale=gs_sb[:, t : t + 1])
+
+        def fetch_whole(t, sent):
+            fetched = buf([P, S], F32, f"fetched{t}")
+            for a in (0, HALF):
+                fetch(sent, fetched[:, a : a + HALF], a, HALF)
+            return fetched
+
+        def deal_words(dealt, picked, first_group, groups):
+            nc.vector.tensor_copy(
+                dealt[:].bitcast(I32).rearrange("p (t g b) -> p t g b", t=4, b=8)[:, :, first_group : first_group + groups, :],
+                picked[:].bitcast(I32).rearrange("p (g t b) -> p t g b", t=4, b=8),
+            )
+
+        sent0 = buf([P, S], F32, "sent0", "ds_table")
+        sent1 = buf([P, S], F32, "sent1")
+        y00 = project(0, 0)
+
+        send(sent0, y00, 0)
+        send(sent1, project(1, 0), 0)
+        send(sent0, project(0, 1), 1)
+        send(sent1, project(1, 1), 1)
+        y20 = project(2, 0)
+        y21 = project(2, 1)
+        y30 = project(3, 0)
+        fetched0 = fetch_whole(0, sent0)
+        take_larger(0, fetched0[:], 0, S)
+        sent2 = buf([P, S], F32, "sent2", "fetched0")
+        send(sent2, y20, 0)
+        fetched1 = fetch_whole(1, sent1)
+        weigh(0, 0, S)
+        take_larger(1, fetched1[:], 0, S)
+        send(sent2, y21, 1)
+        sent3 = buf([P, S], F32, "sent3", "fetched1")
+        send(sent3, y30, 0)
+        halves = []
+        for h in range(2):
+            fetched = buf([P, HALF], F32, f"fetched2{h}")
+            fetch(sent2, fetched[:], h * HALF, HALF)
+            halves.append(fetched)
+        weigh(1, 0, S)
+        for h in range(2):
+            take_larger(2, halves[h][:], h * HALF, HALF)
+        y31 = project(3, 1, "fetched20")
+        ka_picked = buf([P, S], U32, "ka_picked", "fetched21")
+        nc.vector.tensor_copy(ka_picked[:], dw_table[:].bitcast(U32).indirect(l_ka[:]))
+        weigh(2, 0, S)
+        send(sent3, y31, 1)
+
+        d_dealt = [buf([P, S], U32, f"dealt{j}") for j in range(2)]
+        deal_words(d_dealt[0], ka_picked, 0, 16)
+
+        kb_first = buf([P, HALF], U32, "kb_first", "fetched20")
+        nc.vector.tensor_copy(kb_first[:], dw_table[:].bitcast(U32).indirect(entries(l_kb, 0, HALF)))
+        lead = buf([P, QUARTER], F32, "fetched3_lead")
+        fetch(sent3, lead[:], 0, QUARTER)
+        larger_lead = buf([P, QUARTER], F32, "larger_lead")
+        take_larger(3, lead[:], 0, QUARTER, larger_lead[:])
+        weigh(3, 0, QUARTER, larger_lead[:])
+        kb_second = buf([P, HALF], U32, "kb_second", "fetched3_lead")
+        nc.vector.tensor_copy(kb_second[:], dw_table[:].bitcast(U32).indirect(entries(l_kb, HALF, HALF)))
+        deal_words(d_dealt[1], kb_first, 0, 8)
+        rest = buf([P, S - QUARTER], F32, "fetched3_rest", "larger_lead")
+        fetch(sent3, rest[:, 0:QUARTER], QUARTER, QUARTER)
+        fetch(sent3, rest[:, QUARTER:], HALF, HALF)
+
+        def quantise(a, n, tag):
+            words = buf([P, n], U32, f"z_words{a}", tag)
+            plane = buf([P, n], U8, f"z_plane{a}")
+            nc.vector.quantize_mx(out=words[:].bitcast(FP8X4), scales=plane[:], in_=z_bf[:, a : a + n, :].rearrange("p c t -> p (c t)"))
+            return words, plane
+
+        z_lead = quantise(0, QUARTER, None)
+        deal_words(d_dealt[1], kb_second, 8, 8)
+        take_larger(3, rest[:], QUARTER, S - QUARTER)
+
+        def multiply(k, t, z, a, n):
+            h_ps = ps.tile([P, n], F32, name=f"h_ps{k}", tag=f"hbank{k % 4}")
+            for j in range(2):
+                nc.tensor.matmul_mx(
+                    out=h_ps[:],
+                    lhsT=d_dealt[j][:, t * P : (t + 1) * P].bitcast(FP8X4),
+                    lhsT_scale=d_plane[:, j * S + t * P : j * S + (t + 1) * P],
+                    rhs=z[0][:, a : a + n].bitcast(FP8X4),
+                    rhs_scale=z[1][:, a : a + n],
+                    start=(j == 0),
+                    stop=(j == 1),
+                )
+            return h_ps
+
+        def scaled(h_ps, n, name):
+            h_sb = buf([P, n], F32, name)
+            nc.scalar.activation(h_sb[:], h_ps[:], COPY, scale=0.0625)
+            return h_sb
+
+        out_rows = out.rearrange("(g t b) s -> t g b s", t=4, b=8)
+        first = [buf([P, S], F32, f"first{t}") for t in range(4)]
+        second = [buf([P, S], F32, f"second{t}") for t in range(4)]
+
+        def finish(t, a, n, tag, queue):
+            result = buf([P, n], F32, f"result{t}_{a}", tag)
+            nc.vector.tensor_tensor(result[:], first[t][:, a : a + n], second[t][:, a : a + n], MAX)
+            queue.dma_start(out_rows[t][:, :, a : a + n], result[:])
+
+        h_ps = multiply(0, 0, z_lead, 0, QUARTER)
+        h_a = buf([P, QUARTER], F32, "h_lead")
+        nc.vector.tensor_scalar(h_a[:], h_ps[:], 0.0625, None, mybir.AluOpType.mult)
+        weigh(3, QUARTER, S - QUARTER)
+        nc.vector.tensor_copy(first[0][:].indirect(entries(l_n3, 0, QUARTER)), h_a[:])
+        nc.vector.tensor_copy(second[0][:].indirect(entries(l_n4, 0, QUARTER)), h_a[:])
+
+        k = 1
+        pieces = [(t, 0, QUARTER) for t in (1, 2, 3)]
+        pieces = pieces + [(t, a, n) for t in range(4) for a, n in ((QUARTER, QUARTER), (HALF, HALF))]
+        pending = None
+        for t, a, n in pieces:
+            if a == 0:
+                h_ps = multiply(k, t, z_lead, 0, n)
+            else:
+                h_ps = multiply(k, t, z_rest, a - QUARTER, n)
+            h_sb = scaled(h_ps, n, f"h_sb{k}")
+            nc.vector.tensor_copy(first[t][:].indirect(entries(l_n3, a, n)), h_sb[:])
+            nc.vector.tensor_copy(second[t][:].indirect(entries(l_n4, a, n)), h_sb[:])
+            if k == 1:
+                z_rest = quantise(QUARTER, S - QUARTER, f"h_sb{k}")
+            if pending is not None:
+                finish(pending, 0, S, f"h_sb{k}", nc.sync)
+                pending = None
+            if a + n == S and t < 3:
+                pending = t
+            k = k + 1
+        finish(3, 0, HALF, None, nc.sync)
+        finish(3, HALF, HALF, None, nc.scalar)

@@ -1,6 +1,7 @@
 from contextlib import ExitStack
 
 import concourse.mybir as mybir
+from concourse.masks import make_identity
 
 F32 = mybir.dt.float32
 BF16 = mybir.dt.bfloat16
@@ -11,6 +12,7 @@ U8 = mybir.dt.uint8
 FP8X4 = mybir.dt.float8_e4m3fn_x4
 FP4X4 = mybir.dt.float4_e2m1fn_x4
 COPY = mybir.ActivationFunctionType.Copy
+RELU = mybir.ActivationFunctionType.Relu
 MAX = mybir.AluOpType.max
 
 P = 128
@@ -42,24 +44,24 @@ def tile_picked_hdaqrelaysendtwo_none_p_kernel(tc, x_words, x_scales, w1_words, 
             queue.dma_start(t[:].bitcast(I32), rows.unsqueeze(1).to_broadcast([16, 8, TABLE // 4]))
             return t
 
-        def load_word_table(src, name, tag):
-            t = sb.tile([P, TABLE], I32, name=name, tag=tag, align_bytes=64)
-            nc.sync.dma_start(t[:], src[0].rearrange("p n t -> p (n t)").bitcast(I32))
+        def load_word_table(src, name, queue):
+            t = sb.tile([P, TABLE], I32, name=name, tag=name, align_bytes=64)
+            queue.dma_start(t[:], src[0].rearrange("p n t -> p (n t)").bitcast(I32))
             return t
 
         l_offs = load_list(offs, "l_offs")
         xs_table = load_scale_table(x_scales, "xs_table", nc.scalar)
-        l_ka = load_list(ka, "l_ka")
+        w1w_raw = sb.tile([P, 2 * S], U8, name="w1w_raw", align_bytes=64)
+        nc.gpsimd.dma_start(w1w_raw[:].bitcast(I32), w1_words[0].bitcast(I32))
         w1s_raw = sb.tile([P, S], U8, name="w1s_raw", align_bytes=64)
         w1s_rows = w1_scales[0].bitcast(I32).rearrange("(q i) c -> i q c", i=4)
         for i in range(4):
-            nc.gpsimd.dma_start(w1s_raw[i:P:4, :].bitcast(I32), w1s_rows[i].unsqueeze(1).to_broadcast([4, 8, S // 4]))
+            nc.sync.dma_start(w1s_raw[i:P:4, :].bitcast(I32), w1s_rows[i].unsqueeze(1).to_broadcast([4, 8, S // 4]))
         ds_table = load_scale_table(d_scales, "ds_table", nc.scalar)
+        xw_table = load_word_table(x_words, "xw_table", nc.scalar)
+        l_ka = load_list(ka, "l_ka")
         l_kb = load_list(kb, "l_kb")
-        w1w_raw = sb.tile([P, 2 * S], U8, name="w1w_raw", align_bytes=64)
-        nc.scalar.dma_start(w1w_raw[:].bitcast(I32), w1_words[0].bitcast(I32))
         l_n1 = load_list(n1, "l_n1")
-        xw_table = load_word_table(x_words, "xw_table", "xw_table")
 
         xs_picked = sb.tile([P, S], U8, name="xs_picked", tag="xs_picked", align_bytes=64)
         xs_plane = sb.tile([P, S], U8, name="xs_plane", align_bytes=64)
@@ -75,9 +77,9 @@ def tile_picked_hdaqrelaysendtwo_none_p_kernel(tc, x_words, x_scales, w1_words, 
         l_n2 = load_list(n2, "l_n2")
         l_n3 = load_list(n3, "l_n3")
         l_n4 = load_list(n4, "l_n4")
-        dw_table = load_word_table(d_words, "dw_table", "xs_table")
-        gs_sb = sb.tile([P, 4], F32, name="gs_sb", tag="xs_picked", align_bytes=64)
-        nc.sync.dma_start(gs_sb[:], gs.rearrange("(p t) o -> p (t o)", t=4))
+        dw_table = load_word_table(d_words, "dw_table", nc.sync)
+        gs_sb = sb.tile([P, 4], F32, name="gs_sb")
+        nc.gpsimd.dma_start(gs_sb[:], gs.rearrange("(p t) o -> p (t o)", t=4))
 
         xw = sb.tile([P, S], U32, name="xw", align_bytes=64)
         for a in (0, HALF):
@@ -94,7 +96,10 @@ def tile_picked_hdaqrelaysendtwo_none_p_kernel(tc, x_words, x_scales, w1_words, 
         for i in range(1, 4):
             nc.sync.dma_start(d_plane[i:P:32, :].bitcast(I32), d_plane[8 * i : P : 32, :].bitcast(I32))
 
-        y_ps = [ps.tile([P, S], F32, name=f"bank{t}") for t in range(4)]
+        identity = sb.tile([P, P], F32, name="identity")
+        make_identity(nc, identity[:])
+
+        y_ps = [ps.tile([P, S], F32, name=f"y_ps{t}", tag=f"bank{t}") for t in range(4)]
         z_bf = sb.tile([P, S, 4], BF16, name="z_bf", align_bytes=64)
         larger = [sb.tile([P, S], F32, name=f"larger{t}") for t in range(4)]
 
@@ -138,31 +143,31 @@ def tile_picked_hdaqrelaysendtwo_none_p_kernel(tc, x_words, x_scales, w1_words, 
 
         def deal_words(dealt, picked, first_group, groups):
             nc.vector.tensor_copy(
-                dealt[:].bitcast(I32).rearrange("p (t g b) -> p t g b", t=4, b=8)[:, :, first_group : first_group + groups, :],
+                dealt.bitcast(I32).rearrange("p (t g b) -> p t g b", t=4, b=8)[:, :, first_group : first_group + groups, :],
                 picked[:].bitcast(I32).rearrange("p (g t b) -> p t g b", t=4, b=8),
             )
 
         sent0 = buf([P, S], F32, "sent0", "ds_table")
         sent1 = buf([P, S], F32, "sent1")
-        y00 = project(0, 0)
-
-        send(sent0, y00, 0)
+        send(sent0, project(0, 0), 0)
         send(sent1, project(1, 0), 0)
         send(sent0, project(0, 1), 1)
         send(sent1, project(1, 1), 1)
         y20 = project(2, 0)
-        y21 = project(2, 1)
-        y30 = project(3, 0)
         fetched0 = fetch_whole(0, sent0)
         take_larger(0, fetched0[:], 0, S)
-        sent2 = buf([P, S], F32, "sent2", "fetched0")
+        sent2 = buf([P, S], F32, "sent2", "ds_table")
         send(sent2, y20, 0)
         fetched1 = fetch_whole(1, sent1)
+        y21 = project(2, 1, "fetched0")
         weigh(0, 0, S)
         take_larger(1, fetched1[:], 0, S)
         send(sent2, y21, 1)
-        sent3 = buf([P, S], F32, "sent3", "fetched1")
+        y30 = project(3, 0, "fetched1")
+        sent3 = buf([P, S], F32, "sent3")
         send(sent3, y30, 0)
+        ka_picked = buf([P, S], U32, "ka_picked", "fetched0")
+        nc.vector.tensor_copy(ka_picked[:], dw_table[:].bitcast(U32).indirect(l_ka[:]))
         halves = []
         for h in range(2):
             fetched = buf([P, HALF], F32, f"fetched2{h}")
@@ -172,24 +177,23 @@ def tile_picked_hdaqrelaysendtwo_none_p_kernel(tc, x_words, x_scales, w1_words, 
         for h in range(2):
             take_larger(2, halves[h][:], h * HALF, HALF)
         y31 = project(3, 1, "fetched20")
-        ka_picked = buf([P, S], U32, "ka_picked", "fetched21")
-        nc.vector.tensor_copy(ka_picked[:], dw_table[:].bitcast(U32).indirect(l_ka[:]))
+        kb_first = buf([P, HALF], U32, "kb_first", "fetched21")
+        nc.vector.tensor_copy(kb_first[:], dw_table[:].bitcast(U32).indirect(entries(l_kb, 0, HALF)))
         weigh(2, 0, S)
         send(sent3, y31, 1)
 
-        d_dealt = [buf([P, S], U32, f"dealt{j}") for j in range(2)]
-        deal_words(d_dealt[0], ka_picked, 0, 16)
-
-        kb_first = buf([P, HALF], U32, "kb_first", "fetched20")
-        nc.vector.tensor_copy(kb_first[:], dw_table[:].bitcast(U32).indirect(entries(l_kb, 0, HALF)))
+        kb_second = buf([P, HALF], U32, "kb_second", "fetched20")
+        nc.vector.tensor_copy(kb_second[:], dw_table[:].bitcast(U32).indirect(entries(l_kb, HALF, HALF)))
         lead = buf([P, QUARTER], F32, "fetched3_lead")
         fetch(sent3, lead[:], 0, QUARTER)
         larger_lead = buf([P, QUARTER], F32, "larger_lead")
         take_larger(3, lead[:], 0, QUARTER, larger_lead[:])
         weigh(3, 0, QUARTER, larger_lead[:])
-        kb_second = buf([P, HALF], U32, "kb_second", "fetched3_lead")
-        nc.vector.tensor_copy(kb_second[:], dw_table[:].bitcast(U32).indirect(entries(l_kb, HALF, HALF)))
+        dealt_both = buf([P, 2 * S], U32, "dealt_both", "fetched3_lead")
+        d_dealt = [dealt_both[:, j * S : (j + 1) * S] for j in range(2)]
+        deal_words(d_dealt[0], ka_picked, 0, 16)
         deal_words(d_dealt[1], kb_first, 0, 8)
+        deal_words(d_dealt[1], kb_second, 8, 8)
         rest = buf([P, S - QUARTER], F32, "fetched3_rest", "larger_lead")
         fetch(sent3, rest[:, 0:QUARTER], QUARTER, QUARTER)
         fetch(sent3, rest[:, QUARTER:], HALF, HALF)
@@ -201,7 +205,6 @@ def tile_picked_hdaqrelaysendtwo_none_p_kernel(tc, x_words, x_scales, w1_words, 
             return words, plane
 
         z_lead = quantise(0, QUARTER, None)
-        deal_words(d_dealt[1], kb_second, 8, 8)
         take_larger(3, rest[:], QUARTER, S - QUARTER)
 
         def multiply(k, t, z, a, n):
@@ -218,46 +221,66 @@ def tile_picked_hdaqrelaysendtwo_none_p_kernel(tc, x_words, x_scales, w1_words, 
                 )
             return h_ps
 
-        def scaled(h_ps, n, name):
+        def scaled(h_ps, n, name, factor):
             h_sb = buf([P, n], F32, name)
-            nc.scalar.activation(h_sb[:], h_ps[:], COPY, scale=0.0625)
+            nc.scalar.activation(h_sb[:], h_ps[:], COPY, scale=factor)
             return h_sb
 
         out_rows = out.rearrange("(g t b) s -> t g b s", t=4, b=8)
         first = [buf([P, S], F32, f"first{t}") for t in range(4)]
         second = [buf([P, S], F32, f"second{t}") for t in range(4)]
 
-        def finish(t, a, n, tag, queue):
-            result = buf([P, n], F32, f"result{t}_{a}", tag)
+        def turned_sum(name, bank, terms, a, n):
+            acc = ps.tile([P, n], F32, name=name, tag=bank)
+            for c in range(0, n, P):
+                for i, term in enumerate(terms):
+                    nc.tensor.matmul(acc[:, c : c + P], term[:, a + c : a + c + P], identity[:], start=(i == 0), stop=(i == len(terms) - 1), is_transpose=True)
+            return acc
+
+        def finish_on_tensor(t):
+            bank_pairs = (("hbank3", "hbank2"), ("bank0", "bank1"))
+            there, back = bank_pairs[t % 2], bank_pairs[(t + 1) % 2]
+            minus_first_t = turned_sum(f"minus_first_t{t}", there[0], [first[t]], 0, S)
+            excess_t = turned_sum(f"excess_t{t}", there[1], [second[t], first[t]], 0, S)
+            first_t = buf([P, S], F32, f"first_t{t}")
+            nc.scalar.activation(first_t[:], minus_first_t[:], COPY, scale=-1.0)
+            gain_t = buf([P, S], F32, f"gain_t{t}")
+            nc.scalar.activation(gain_t[:], excess_t[:], RELU)
+            result = buf([P, S], F32, f"result{t}")
+            for h in range(2):
+                total = turned_sum(f"total{t}{h}", back[h], [first_t, gain_t], h * HALF, HALF)
+                nc.scalar.activation(result[:, h * HALF : (h + 1) * HALF], total[:], COPY)
+            nc.sync.dma_start(out_rows[t], result[:])
+
+        def finish_on_vector(t, a, n, queue):
+            result = buf([P, n], F32, f"result{t}_{a}")
             nc.vector.tensor_tensor(result[:], first[t][:, a : a + n], second[t][:, a : a + n], MAX)
             queue.dma_start(out_rows[t][:, :, a : a + n], result[:])
 
         h_ps = multiply(0, 0, z_lead, 0, QUARTER)
-        h_a = buf([P, QUARTER], F32, "h_lead")
-        nc.vector.tensor_scalar(h_a[:], h_ps[:], 0.0625, None, mybir.AluOpType.mult)
+        h_minus = buf([P, QUARTER], F32, "h_lead_minus")
+        nc.vector.tensor_scalar(h_minus[:], h_ps[:], -0.0625, None, mybir.AluOpType.mult)
+        h_plus = scaled(h_ps, QUARTER, "h_lead_plus", 0.0625)
         weigh(3, QUARTER, S - QUARTER)
-        nc.vector.tensor_copy(first[0][:].indirect(entries(l_n3, 0, QUARTER)), h_a[:])
-        nc.vector.tensor_copy(second[0][:].indirect(entries(l_n4, 0, QUARTER)), h_a[:])
+        nc.vector.tensor_copy(first[0][:].indirect(entries(l_n3, 0, QUARTER)), h_minus[:])
+        nc.vector.tensor_copy(second[0][:].indirect(entries(l_n4, 0, QUARTER)), h_plus[:])
 
         k = 1
         pieces = [(t, 0, QUARTER) for t in (1, 2, 3)]
         pieces = pieces + [(t, a, n) for t in range(4) for a, n in ((QUARTER, QUARTER), (HALF, HALF))]
-        pending = None
         for t, a, n in pieces:
             if a == 0:
                 h_ps = multiply(k, t, z_lead, 0, n)
             else:
                 h_ps = multiply(k, t, z_rest, a - QUARTER, n)
-            h_sb = scaled(h_ps, n, f"h_sb{k}")
-            nc.vector.tensor_copy(first[t][:].indirect(entries(l_n3, a, n)), h_sb[:])
-            nc.vector.tensor_copy(second[t][:].indirect(entries(l_n4, a, n)), h_sb[:])
+            h_minus = scaled(h_ps, n, f"h_minus{k}", -0.0625 if t < 3 else 0.0625)
+            h_plus = scaled(h_ps, n, f"h_plus{k}", 0.0625) if t < 3 else h_minus
+            nc.vector.tensor_copy(first[t][:].indirect(entries(l_n3, a, n)), h_minus[:])
             if k == 1:
-                z_rest = quantise(QUARTER, S - QUARTER, f"h_sb{k}")
-            if pending is not None:
-                finish(pending, 0, S, f"h_sb{k}", nc.sync)
-                pending = None
-            if a + n == S and t < 3:
-                pending = t
+                z_rest = quantise(QUARTER, S - QUARTER, "h_lead_plus")
+            nc.vector.tensor_copy(second[t][:].indirect(entries(l_n4, a, n)), h_plus[:])
             k = k + 1
-        finish(3, 0, HALF, None, nc.sync)
-        finish(3, HALF, HALF, None, nc.scalar)
+        for t in range(3):
+            finish_on_tensor(t)
+        finish_on_vector(3, 0, HALF, nc.sync)
+        finish_on_vector(3, HALF, HALF, nc.scalar)

@@ -49,8 +49,12 @@ def tile_picked_hdaqrelaysendtwo_none_p_kernel(tc, x_words, x_scales, w1_words, 
             queue.dma_start(t[:], src[0].rearrange("p n t -> p (n t)").bitcast(I32))
             return t
 
+        identity = sb.tile([P, P], F32, name="identity")
+        make_identity(nc, identity[:])
+
         l_offs = load_list(offs, "l_offs")
         xs_table = load_scale_table(x_scales, "xs_table", nc.scalar)
+        l_ka = load_list(ka, "l_ka")
         w1w_raw = sb.tile([P, 2 * S], U8, name="w1w_raw", align_bytes=64)
         nc.gpsimd.dma_start(w1w_raw[:].bitcast(I32), w1_words[0].bitcast(I32))
         w1s_raw = sb.tile([P, S], U8, name="w1s_raw", align_bytes=64)
@@ -59,7 +63,6 @@ def tile_picked_hdaqrelaysendtwo_none_p_kernel(tc, x_words, x_scales, w1_words, 
             nc.sync.dma_start(w1s_raw[i:P:4, :].bitcast(I32), w1s_rows[i].unsqueeze(1).to_broadcast([4, 8, S // 4]))
         ds_table = load_scale_table(d_scales, "ds_table", nc.scalar)
         xw_table = load_word_table(x_words, "xw_table", nc.scalar)
-        l_ka = load_list(ka, "l_ka")
         l_kb = load_list(kb, "l_kb")
         l_n1 = load_list(n1, "l_n1")
 
@@ -95,9 +98,6 @@ def tile_picked_hdaqrelaysendtwo_none_p_kernel(tc, x_words, x_scales, w1_words, 
             )
         for i in range(1, 4):
             nc.sync.dma_start(d_plane[i:P:32, :].bitcast(I32), d_plane[8 * i : P : 32, :].bitcast(I32))
-
-        identity = sb.tile([P, P], F32, name="identity")
-        make_identity(nc, identity[:])
 
         y_ps = [ps.tile([P, S], F32, name=f"y_ps{t}", tag=f"bank{t}") for t in range(4)]
         z_bf = sb.tile([P, S, 4], BF16, name="z_bf", align_bytes=64)
@@ -250,7 +250,7 @@ def tile_picked_hdaqrelaysendtwo_none_p_kernel(tc, x_words, x_scales, w1_words, 
             for h in range(2):
                 total = turned_sum(f"total{t}{h}", back[h], [first_t, gain_t], h * HALF, HALF)
                 nc.scalar.activation(result[:, h * HALF : (h + 1) * HALF], total[:], COPY)
-            nc.sync.dma_start(out_rows[t], result[:])
+            nc.scalar.dma_start(out_rows[t], result[:])
 
         def finish_on_vector(t, a, n, queue):
             result = buf([P, n], F32, f"result{t}_{a}")
@@ -260,7 +260,8 @@ def tile_picked_hdaqrelaysendtwo_none_p_kernel(tc, x_words, x_scales, w1_words, 
         h_ps = multiply(0, 0, z_lead, 0, QUARTER)
         h_minus = buf([P, QUARTER], F32, "h_lead_minus")
         nc.vector.tensor_scalar(h_minus[:], h_ps[:], -0.0625, None, mybir.AluOpType.mult)
-        h_plus = scaled(h_ps, QUARTER, "h_lead_plus", 0.0625)
+        h_plus = buf([P, QUARTER], F32, "h_lead_plus")
+        nc.vector.tensor_scalar(h_plus[:], h_ps[:], 0.0625, None, mybir.AluOpType.mult)
         weigh(3, QUARTER, S - QUARTER)
         nc.vector.tensor_copy(first[0][:].indirect(entries(l_n3, 0, QUARTER)), h_minus[:])
         nc.vector.tensor_copy(second[0][:].indirect(entries(l_n4, 0, QUARTER)), h_plus[:])
@@ -277,10 +278,10 @@ def tile_picked_hdaqrelaysendtwo_none_p_kernel(tc, x_words, x_scales, w1_words, 
             h_plus = scaled(h_ps, n, f"h_plus{k}", 0.0625) if t < 3 else h_minus
             nc.vector.tensor_copy(first[t][:].indirect(entries(l_n3, a, n)), h_minus[:])
             if k == 1:
-                z_rest = quantise(QUARTER, S - QUARTER, "h_lead_plus")
+                z_rest = quantise(QUARTER, S - QUARTER, "h_lead_minus")
             nc.vector.tensor_copy(second[t][:].indirect(entries(l_n4, a, n)), h_plus[:])
             k = k + 1
         for t in range(3):
             finish_on_tensor(t)
         finish_on_vector(3, 0, HALF, nc.sync)
-        finish_on_vector(3, HALF, HALF, nc.scalar)
+        finish_on_vector(3, HALF, HALF, nc.sync)

from contextlib import ExitStack

import concourse.mybir as mybir
from concourse.masks import make_identity

F32 = mybir.dt.float32
BF16 = mybir.dt.bfloat16
I32 = mybir.dt.int32
U32 = mybir.dt.uint32
U16 = mybir.dt.uint16
U8 = mybir.dt.uint8
FP8X4 = mybir.dt.float8_e4m3fn_x4
FP4X4 = mybir.dt.float4_e2m1fn_x4
COPY = mybir.ActivationFunctionType.Copy
RELU = mybir.ActivationFunctionType.Relu
MAX = mybir.AluOpType.max

P = 128
S = 512
TABLE = 2048
HALF = 256
QUARTER = 128
FLOPS = 3 * 2 * 512 * 512 * 512


def tile_picked_hdaqrelaysendtwo_none_p_kernel(tc, x_words, x_scales, w1_words, w1_scales, gs, d_words, d_scales, offs, n1, n2, ka, kb, n3, n4, out):
    nc = tc.nc
    with ExitStack() as ctx:
        lists = ctx.enter_context(tc.tile_pool(name="lists", bufs=1))
        sb = ctx.enter_context(tc.tile_pool(name="sb", bufs=1))
        ps = ctx.enter_context(tc.psum_pool(name="ps", bufs=1))

        def load_list(src, name):
            t = lists.tile([P, S // 16], U16, name=name)
            nc.sync.dma_start(t[:], src)
            return t

        def entries(lst, a, n):
            return lst[:, a // 16 : (a + n) // 16]

        def load_scale_table(src, name, queue):
            t = sb.tile([P, TABLE], U8, name=name, tag=name, align_bytes=64)
            rows = src[0].bitcast(I32)
            queue.dma_start(t[:].bitcast(I32), rows.unsqueeze(1).to_broadcast([16, 8, TABLE // 4]))
            return t

        def load_word_table(src, name, queue):
            t = sb.tile([P, TABLE], I32, name=name, tag=name, align_bytes=64)
            queue.dma_start(t[:], src[0].rearrange("p n t -> p (n t)").bitcast(I32))
            return t

        identity = sb.tile([P, P], F32, name="identity")
        make_identity(nc, identity[:])

        l_offs = load_list(offs, "l_offs")
        xs_table = load_scale_table(x_scales, "xs_table", nc.scalar)
        l_ka = load_list(ka, "l_ka")
        w1w_raw = sb.tile([P, 2 * S], U8, name="w1w_raw", align_bytes=64)
        nc.gpsimd.dma_start(w1w_raw[:].bitcast(I32), w1_words[0].bitcast(I32))
        w1s_raw = sb.tile([P, S], U8, name="w1s_raw", align_bytes=64)
        w1s_rows = w1_scales[0].bitcast(I32).rearrange("(q i) c -> i q c", i=4)
        for i in range(4):
            nc.sync.dma_start(w1s_raw[i:P:4, :].bitcast(I32), w1s_rows[i].unsqueeze(1).to_broadcast([4, 8, S // 4]))
        ds_table = load_scale_table(d_scales, "ds_table", nc.scalar)
        xw_table = load_word_table(x_words, "xw_table", nc.scalar)
        l_kb = load_list(kb, "l_kb")
        l_n1 = load_list(n1, "l_n1")

        xs_picked = sb.tile([P, S], U8, name="xs_picked", tag="xs_picked", align_bytes=64)
        xs_plane = sb.tile([P, S], U8, name="xs_plane", align_bytes=64)
        nc.vector.memset(xs_plane[:].bitcast(I32), 0)
        nc.vector.tensor_copy(xs_picked[:], xs_table[:].indirect(l_offs[:]))
        w1w = sb.tile([P, 2 * S], U8, name="w1w", align_bytes=64)
        for i in range(4):
            nc.scalar.dma_start(xs_plane[i:P:32, :].bitcast(I32), xs_picked[8 * i : P : 32, :].bitcast(I32))
        nc.scalar.copy(w1w[:].bitcast(U16).rearrange("p (t m) -> p t m", t=4), w1w_raw[:].bitcast(U16).rearrange("p (m t) -> p t m", t=4))
        w1s = sb.tile([P, S], U8, name="w1s", align_bytes=64)
        nc.vector.tensor_copy(w1s[:].rearrange("p (t m) -> p m t", t=4), w1s_raw[:].rearrange("p (m t) -> p m t", t=4))

        l_n2 = load_list(n2, "l_n2")
        l_n3 = load_list(n3, "l_n3")
        l_n4 = load_list(n4, "l_n4")
        dw_table = load_word_table(d_words, "dw_table", nc.sync)
        gs_sb = sb.tile([P, 4], F32, name="gs_sb")
        nc.gpsimd.dma_start(gs_sb[:], gs.rearrange("(p t) o -> p (t o)", t=4))

        xw = sb.tile([P, S], U32, name="xw", align_bytes=64)
        for a in (0, HALF):
            nc.vector.tensor_copy(xw[:, a : a + HALF], xw_table[:].bitcast(U32).indirect(entries(l_offs, a, HALF)))

        d_plane = sb.tile([P, 2 * S], U8, name="d_plane", align_bytes=64)
        for j, lst in enumerate((l_ka, l_kb)):
            picked = sb.tile([P, S], U8, name=f"ds_picked{j}", tag=("ds_picked0", "xw_table")[j], align_bytes=64)
            nc.vector.tensor_copy(picked[:], ds_table[:].indirect(lst[:]))
            nc.vector.tensor_copy(
                d_plane[:, j * S : (j + 1) * S].bitcast(I32).rearrange("p (t g b) -> p t g b", t=4, b=2),
                picked[:].bitcast(I32).rearrange("p (g t b) -> p t g b", t=4, b=2),
            )
        for i in range(1, 4):
            nc.sync.dma_start(d_plane[i:P:32, :].bitcast(I32), d_plane[8 * i : P : 32, :].bitcast(I32))

        y_ps = [ps.tile([P, S], F32, name=f"y_ps{t}", tag=f"bank{t}") for t in range(4)]
        z_bf = sb.tile([P, S, 4], BF16, name="z_bf", align_bytes=64)
        larger = [sb.tile([P, S], F32, name=f"larger{t}") for t in range(4)]

        def buf(shape, dtype, name, tag=None):
            return sb.tile(shape, dtype, name=name, tag=tag or name, align_bytes=64)

        def project(t, h, tag=None):
            cols = slice(h * HALF, (h + 1) * HALF)
            nc.tensor.matmul_mx(
                out=y_ps[t][:, cols],
                lhsT=w1w[:, t * 256 : (t + 1) * 256].bitcast(FP4X4),
                lhsT_scale=w1s[:, t * P : (t + 1) * P],
                rhs=xw[:, cols].bitcast(FP8X4),
                rhs_scale=xs_plane[:, cols],
                start=True,
                stop=True,
            )
            y_sb = buf([P, HALF], F32, f"y{t}{h}", tag)
            nc.scalar.activation(y_sb[:], y_ps[t][:, cols], COPY)
            return y_sb

        def send(sent, y_sb, h):
            nc.vector.tensor_copy(sent[:].indirect(entries(l_n1, h * HALF, HALF)), y_sb[:])

        def fetch(sent, dst, a, n):
            nc.scalar.activation(dst, sent[:].indirect(entries(l_n2, a, n)), COPY)

        def take_larger(t, fetched, a, n, dst=None):
            dst = larger[t][:, a : a + n] if dst is None else dst
            nc.vector.tensor_tensor(dst, fetched, y_ps[t][:, a : a + n], MAX)

        def weigh(t, a, n, src=None):
            src = larger[t][:, a : a + n] if src is None else src
            nc.scalar.activation(z_bf[:, a : a + n, t], src, COPY, scale=gs_sb[:, t : t + 1])

        def fetch_whole(t, sent):
            fetched = buf([P, S], F32, f"fetched{t}")
            for a in (0, HALF):
                fetch(sent, fetched[:, a : a + HALF], a, HALF)
            return fetched

        def deal_words(dealt, picked, first_group, groups):
            nc.vector.tensor_copy(
                dealt.bitcast(I32).rearrange("p (t g b) -> p t g b", t=4, b=8)[:, :, first_group : first_group + groups, :],
                picked[:].bitcast(I32).rearrange("p (g t b) -> p t g b", t=4, b=8),
            )

        sent0 = buf([P, S], F32, "sent0", "ds_table")
        sent1 = buf([P, S], F32, "sent1")
        send(sent0, project(0, 0), 0)
        send(sent1, project(1, 0), 0)
        send(sent0, project(0, 1), 1)
        send(sent1, project(1, 1), 1)
        y20 = project(2, 0)
        fetched0 = fetch_whole(0, sent0)
        take_larger(0, fetched0[:], 0, S)
        sent2 = buf([P, S], F32, "sent2", "ds_table")
        send(sent2, y20, 0)
        fetched1 = fetch_whole(1, sent1)
        y21 = project(2, 1, "fetched0")
        weigh(0, 0, S)
        take_larger(1, fetched1[:], 0, S)
        send(sent2, y21, 1)
        y30 = project(3, 0, "fetched1")
        sent3 = buf([P, S], F32, "sent3")
        send(sent3, y30, 0)
        ka_picked = buf([P, S], U32, "ka_picked", "fetched0")
        nc.vector.tensor_copy(ka_picked[:], dw_table[:].bitcast(U32).indirect(l_ka[:]))
        halves = []
        for h in range(2):
            fetched = buf([P, HALF], F32, f"fetched2{h}")
            fetch(sent2, fetched[:], h * HALF, HALF)
            halves.append(fetched)
        weigh(1, 0, S)
        for h in range(2):
            take_larger(2, halves[h][:], h * HALF, HALF)
        y31 = project(3, 1, "fetched20")
        kb_first = buf([P, HALF], U32, "kb_first", "fetched21")
        nc.vector.tensor_copy(kb_first[:], dw_table[:].bitcast(U32).indirect(entries(l_kb, 0, HALF)))
        weigh(2, 0, S)
        send(sent3, y31, 1)

        kb_second = buf([P, HALF], U32, "kb_second", "fetched20")
        nc.vector.tensor_copy(kb_second[:], dw_table[:].bitcast(U32).indirect(entries(l_kb, HALF, HALF)))
        lead = buf([P, QUARTER], F32, "fetched3_lead")
        fetch(sent3, lead[:], 0, QUARTER)
        larger_lead = buf([P, QUARTER], F32, "larger_lead")
        take_larger(3, lead[:], 0, QUARTER, larger_lead[:])
        weigh(3, 0, QUARTER, larger_lead[:])
        dealt_both = buf([P, 2 * S], U32, "dealt_both", "fetched3_lead")
        d_dealt = [dealt_both[:, j * S : (j + 1) * S] for j in range(2)]
        deal_words(d_dealt[0], ka_picked, 0, 16)
        deal_words(d_dealt[1], kb_first, 0, 8)
        deal_words(d_dealt[1], kb_second, 8, 8)
        rest = buf([P, S - QUARTER], F32, "fetched3_rest", "larger_lead")
        fetch(sent3, rest[:, 0:QUARTER], QUARTER, QUARTER)
        fetch(sent3, rest[:, QUARTER:], HALF, HALF)

        def quantise(a, n, tag):
            words = buf([P, n], U32, f"z_words{a}", tag)
            plane = buf([P, n], U8, f"z_plane{a}")
            nc.vector.quantize_mx(out=words[:].bitcast(FP8X4), scales=plane[:], in_=z_bf[:, a : a + n, :].rearrange("p c t -> p (c t)"))
            return words, plane

        z_lead = quantise(0, QUARTER, None)
        take_larger(3, rest[:], QUARTER, S - QUARTER)

        def multiply(k, t, z, a, n):
            h_ps = ps.tile([P, n], F32, name=f"h_ps{k}", tag=f"hbank{k % 4}")
            for j in range(2):
                nc.tensor.matmul_mx(
                    out=h_ps[:],
                    lhsT=d_dealt[j][:, t * P : (t + 1) * P].bitcast(FP8X4),
                    lhsT_scale=d_plane[:, j * S + t * P : j * S + (t + 1) * P],
                    rhs=z[0][:, a : a + n].bitcast(FP8X4),
                    rhs_scale=z[1][:, a : a + n],
                    start=(j == 0),
                    stop=(j == 1),
                )
            return h_ps

        def scaled(h_ps, n, name, factor):
            h_sb = buf([P, n], F32, name)
            nc.scalar.activation(h_sb[:], h_ps[:], COPY, scale=factor)
            return h_sb

        out_rows = out.rearrange("(g t b) s -> t g b s", t=4, b=8)
        first = [buf([P, S], F32, f"first{t}") for t in range(4)]
        second = [buf([P, S], F32, f"second{t}") for t in range(4)]

        def turned_sum(name, bank, terms, a, n):
            acc = ps.tile([P, n], F32, name=name, tag=bank)
            for c in range(0, n, P):
                for i, term in enumerate(terms):
                    nc.tensor.matmul(acc[:, c : c + P], term[:, a + c : a + c + P], identity[:], start=(i == 0), stop=(i == len(terms) - 1), is_transpose=True)
            return acc

        def finish_on_tensor(t):
            bank_pairs = (("hbank3", "hbank2"), ("bank0", "bank1"))
            there, back = bank_pairs[t % 2], bank_pairs[(t + 1) % 2]
            minus_first_t = turned_sum(f"minus_first_t{t}", there[0], [first[t]], 0, S)
            excess_t = turned_sum(f"excess_t{t}", there[1], [second[t], first[t]], 0, S)
            first_t = buf([P, S], F32, f"first_t{t}")
            nc.scalar.activation(first_t[:], minus_first_t[:], COPY, scale=-1.0)
            gain_t = buf([P, S], F32, f"gain_t{t}")
            nc.scalar.activation(gain_t[:], excess_t[:], RELU)
            result = buf([P, S], F32, f"result{t}")
            for h in range(2):
                total = turned_sum(f"total{t}{h}", back[h], [first_t, gain_t], h * HALF, HALF)
                nc.scalar.activation(result[:, h * HALF : (h + 1) * HALF], total[:], COPY)
            nc.scalar.dma_start(out_rows[t], result[:])

        def finish_on_vector(t, a, n, queue):
            result = buf([P, n], F32, f"result{t}_{a}")
            nc.vector.tensor_tensor(result[:], first[t][:, a : a + n], second[t][:, a : a + n], MAX)
            queue.dma_start(out_rows[t][:, :, a : a + n], result[:])

        h_ps = multiply(0, 0, z_lead, 0, QUARTER)
        h_minus = buf([P, QUARTER], F32, "h_lead_minus")
        nc.vector.tensor_scalar(h_minus[:], h_ps[:], -0.0625, None, mybir.AluOpType.mult)
        h_plus = buf([P, QUARTER], F32, "h_lead_plus")
        nc.vector.tensor_scalar(h_plus[:], h_ps[:], 0.0625, None, mybir.AluOpType.mult)
        weigh(3, QUARTER, S - QUARTER)
        nc.vector.tensor_copy(first[0][:].indirect(entries(l_n3, 0, QUARTER)), h_minus[:])
        nc.vector.tensor_copy(second[0][:].indirect(entries(l_n4, 0, QUARTER)), h_plus[:])

        k = 1
        pieces = [(t, 0, QUARTER) for t in (1, 2, 3)]
        pieces = pieces + [(t, a, n) for t in range(4) for a, n in ((QUARTER, QUARTER), (HALF, HALF))]
        for t, a, n in pieces:
            if a == 0:
                h_ps = multiply(k, t, z_lead, 0, n)
            else:
                h_ps = multiply(k, t, z_rest, a - QUARTER, n)
            h_minus = scaled(h_ps, n, f"h_minus{k}", -0.0625 if t < 3 else 0.0625)
            h_plus = scaled(h_ps, n, f"h_plus{k}", 0.0625) if t < 3 else h_minus
            nc.vector.tensor_copy(first[t][:].indirect(entries(l_n3, a, n)), h_minus[:])
            if k == 1:
                z_rest = quantise(QUARTER, S - QUARTER, "h_lead_minus")
            nc.vector.tensor_copy(second[t][:].indirect(entries(l_n4, a, n)), h_plus[:])
            k = k + 1
        for t in range(3):
            finish_on_tensor(t)
        finish_on_vector(3, 0, HALF, nc.sync)
        finish_on_vector(3, HALF, HALF, nc.sync)
